import numpy as np, ml_dtypes
CORES = [2,3,42,43,82,83,122,123]
N = 8
import mx_ref
NC, G = 512, 4
C, C2 = np.float32(0.043), np.float32(0.047)
CNT = [[64,64,64,64,64,64,64,64],[64,64,64,64,64,64,64,64],[64,64,64,64,64,64,64,64],[64,64,64,64,64,64,64,64],[64,64,64,64,64,64,64,64],[64,64,64,64,64,64,64,64],[64,64,64,64,64,64,64,64],[64,64,64,64,64,64,64,64]]
OFF = [[sum(c[:e]) for e in range(N + 1)] for c in CNT]
BF = ml_dtypes.bfloat16
def cut(t, i, w=512):
    return t[:, w * i:w * i + w]
def tile(rs):
    return np.stack(rs, axis=2).reshape(128, -1).astype(BF)
def layer(w, X):
    out = []
    for i in range(G):
        for t in range(len(X)):
            p = mx_ref.matmul(mx_ref.quantize(cut(w, len(X) * i + t)), X[t])
            z = p if t == 0 else z + p
        out.append(z)
    return out
def act(Z):
    return [np.maximum(z, 0) * C for z in Z]
def setup_inputs(rng):
    def f(*shape):
        return mx_ref.flush((rng.standard_normal(shape, dtype=np.float32) * np.exp2(rng.integers(-2, 3, shape[:-1] + (1,)))).astype(BF))
    return {"x": f(N, 128, 4 * NC), "w1": f(N, 128, G * 512), "w2": f(N, 128, G * 512), "w3": f(N, 128, 512)}
def setup_inputs_blocks(rng):
    d = setup_inputs(rng)
    for k in ("x", "w3"): d[k] = mx_ref.spread(d[k], rng, 4)
    for k in ("w1", "w2"): d[k] = mx_ref.spread(d[k], rng, 2)
    return d
def setup_inputs_wide(rng):
    d = setup_inputs(rng)
    for k in ("x", "w1", "w2", "w3"): d[k] = mx_ref.flush((d[k].astype(np.float32) * np.exp2(rng.integers(-4, 5, (N, 1, 1))).astype(np.float32)).astype(BF))
    return d
def setup_inputs_zeros(rng):
    d = setup_inputs(rng); v = d["x"].reshape(N, 128, -1, 4).copy()
    v[np.broadcast_to((rng.random((N, 1, v.shape[2], 1)) < 0.33), v.shape)] = 0
    d["x"] = v.reshape(d["x"].shape)
    return d
def act2(Z):
    return [np.maximum(z, 0) * C2 for z in Z]
def reference(x, w1, w2, w3):
    h = [tile(act(layer(w1[j], [mx_ref.quantize(x[j])]))) for j in range(N)]
    g = []
    for e in range(N):
        t = np.concatenate([h[j][:, 4 * OFF[j][e]:4 * OFF[j][e + 1]] for j in range(N)], axis=1)
        g.append(tile(act2(layer(w2[e], [mx_ref.quantize(t)]))))
    y = np.zeros((N, 128, NC), np.float32)
    for j in range(N):
        back = []
        for e in range(N):
            a = sum(CNT[i][e] for i in range(j))
            back.append(g[e][:, 4 * a:4 * a + 4 * CNT[j][e]])
        y[j] = mx_ref.matmul(mx_ref.quantize(w3[j]), mx_ref.quantize(np.concatenate(back, axis=1)))
    return {"y": y}

@@ -1,0 +1,222 @@
+import numpy as np
+from concourse.bass import DstId, RemoteDMATransfer
+from concourse.mybir import dt, AluOpType, ActivationFunctionType
+
+F8 = "float8_e4m3fn_x4"
+SCRATCH = {
+    "xs": ("sbuf", [128, 2048], "bfloat16"),
+    "w1s": ("sbuf", [128, 2048], "bfloat16"),
+    "w2s": ("sbuf", [128, 2048], "bfloat16"),
+    "w3s": ("sbuf", [128, 512], "bfloat16"),
+    "h": ("sbuf", [128, 2048], "bfloat16"),
+    "gt": ("sbuf", [128, 2048], "bfloat16"),
+    "ys": ("sbuf", [128, 512], "float32"),
+    "qx": ("sbuf", [128, 512], F8), "sx": ("sbuf", [128, 512], "uint8"),
+    "qw1": ("sbuf", [128, 512], F8), "sw1": ("sbuf", [128, 512], "uint8"),
+    "qw2": ("sbuf", [128, 512], F8), "sw2": ("sbuf", [128, 512], "uint8"),
+    "qw3": ("sbuf", [128, 128], F8), "sw3": ("sbuf", [128, 128], "uint8"),
+    "qf": ("sbuf", [128, 256], F8), "sf": ("sbuf", [128, 256], "uint8"),
+    "qn": ("sbuf", [128, 128], F8), "sn": ("sbuf", [128, 128], "uint8"),
+    "qb": ("sbuf", [128, 576], F8), "sb": ("sbuf", [128, 576], "uint8"),
+    "qgf": ("sbuf", [128, 256], F8), "sgf": ("sbuf", [128, 256], "uint8"),
+    "qa": ("sbuf", [128, 704], F8), "sa": ("sbuf", [128, 704], "uint8"),
+    "ps": ("psum", [128, 4096], "float32"),
+}
+SEMAPHORES = ["lx0", "lx1", "lw1a", "lw1b", "lw2", "lw3", "qv", "mm", "es", "ev", "sent",
+              "far1", "near1", "far2", "near2", "store"]
+
+
+def rank_program(g, core, T, topo):
+    rank = T.rank_of(core)
+    if rank is None:
+        return
+    S = T.sem
+    W = int(T.tables["CNT"][0][0])
+    cores = T.cores
+    chips = []
+    for c in cores:
+        if topo.chip(c) not in chips:
+            chips.append(topo.chip(c))
+    members = [[r for r in range(len(cores)) if topo.chip(cores[r]) == ch] for ch in chips]
+
+    def place(r):
+        a = chips.index(topo.chip(cores[r]))
+        return a, members[a].index(r)
+
+    def far_of(r):
+        base = 2 * (1 - place(r)[0] // 2)
+        return members[base] + members[base + 1]
+
+    def near_of(r):
+        return members[place(r)[0] ^ 1]
+
+    a, slot = place(rank)
+    far, near, partner = far_of(rank), near_of(rank), members[a][1 - slot]
+
+    def b_col(r, o):
+        s = place(r)[1]
+        if o in far_of(r):
+            return (0 if s == 0 else 5 * W) + W * far_of(r).index(o)
+        if o in near_of(r):
+            return (4 * W if s == 0 else 3 * W) + W * near_of(r).index(o)
+        return 6 * W if s == 0 else 2 * W
+
+    def a_col(r, o):
+        s = place(r)[1]
+        if o in far_of(r):
+            return (7 * W if s == 0 else 0) + W * far_of(r).index(o)
+        if o in near_of(r):
+            return (5 * W if s == 0 else 4 * W) + W * near_of(r).index(o)
+        return 4 * W if s == 0 else 6 * W
+
+    bpair = 7 * W if slot == 0 else 0
+    bfar, bnear = (0, 4 * W) if slot == 0 else (5 * W, W)
+    apiece = 0 if slot == 0 else 7 * W
+    afar, anear = (7 * W, 3 * W) if slot == 0 else (0, 4 * W)
+
+    def bits(m):
+        return [1 << i for i in range(16) if m >> i & 1]
+    off = bits(topo.mask(core, cores[far[0]]))
+    on = [b for b in bits(topo.mask(core, cores[partner])) if b not in off]
+
+    def share(engines, k, n):
+        w = len(engines) // n
+        return sum(engines[k * w:k * w + w])
+
+    sent = [0]
+
+    def send(moves, sem):
+        for part in (0, 1):
+            tr = []
+            for d, mask, src, sc, dst, dc in moves:
+                rid, pid, _ = topo.addr(cores[d])
+                s, t = T[src[part]][:, sc:sc + W], T[dst[part]][:, dc:dc + W]
+                if part == 0:
+                    s, t = s.bitcast(dt.uint8), t.bitcast(dt.uint8)
+                tr.append(RemoteDMATransfer(dst_ids=[DstId(rid=rid, pnc=pid)], dma_engine_mask=mask,
+                                            remote_sem=sem, src=s, dst=t))
+                sent[0] += len(bits(mask))
+            g.remote_dma_fused(tr, local_sem=S.sent)
+
+    fx = 4 * W * far[0]
+    nx = 4 * W * min(members[a][0], near[0])
+    g.sync.dma_start(T.xs[:, 0:1024], T.x[:, fx:fx + 1024]).then_inc(S.lx0, 16)
+    g.scalar.dma_start(T.w1s[:, 0:1024], T.w1[:, 0:1024]).then_inc(S.lw1a, 16)
+    g.sync.dma_start(T.w1s[:, 1024:2048], T.w1[:, 1024:2048]).then_inc(S.lw1b, 16)
+    g.scalar.dma_start(T.xs[:, 1024:2048], T.x[:, nx:nx + 1024]).then_inc(S.lx1, 16)
+    g.sync.dma_start(T.w2s[:], T.w2[:]).then_inc(S.lw2, 16)
+    g.scalar.dma_start(T.w3s[:], T.w3[:]).then_inc(S.lw3, 16)
+
+    nq, nm, ns, nv = [0], [0], [0], [0]
+
+    def quant(codes, scales, src):
+        g.vector.quantize_mx(codes, scales, src).then_inc(S.qv, 1)
+        nq[0] += 1
+        return nq[0]
+
+    def products(w, sw, x, sx, c, bank):
+        for i in range(4):
+            p = 512 * (bank + i)
+            g.tensor.matmul_mx(T.ps[:, p:p + 256], w[:, 128 * i:128 * i + 128], sw[:, 128 * i:128 * i + 128],
+                               x[:, c:c + 256], sx[:, c:c + 256], True, True).then_inc(S.mm, 1)
+
+    def empty(t, lo, bank, m0, c):
+        for i in (0, 2):
+            p = 512 * (bank + i)
+            g.scalar.wait_ge(S.mm, m0 + i + 1)
+            g.scalar.activation(t[:, lo + i:lo + 1024:4], T.ps[:, p:p + 256], ActivationFunctionType.Relu,
+                                scale=c).then_inc(S.es, 1)
+            ns[0] += 1
+        for i in (1, 3):
+            p = 512 * (bank + i)
+            g.vector.wait_ge(S.mm, m0 + i + 1)
+            g.vector.tensor_scalar(t[:, lo + i:lo + 1024:4], T.ps[:, p:p + 256], 0.0, c, AluOpType.max,
+                                   AluOpType.mult).then_inc(S.ev, 1)
+            nv[0] += 1
+        g.vector.wait_ge(S.es, ns[0])
+        g.vector.wait_ge(S.ev, nv[0])
+
+    c1, c2 = float(np.float32(0.043)), float(np.float32(0.047))
+    H, G = T.h, T.gt
+
+    g.vector.wait_ge(S.lx0, 16)
+    quant(T.qx[:, 0:256], T.sx[:, 0:256], T.xs[:, 0:1024])
+    g.vector.wait_ge(S.lw1a, 16)
+    k_a = quant(T.qw1[:, 0:256], T.sw1[:, 0:256], T.w1s[:, 0:1024])
+    g.vector.wait_ge(S.lw1b, 16)
+    k_b = quant(T.qw1[:, 256:512], T.sw1[:, 256:512], T.w1s[:, 1024:2048])
+    empty(H, 0, 0, 0, c1)
+    k_h0 = quant(T.qf[:], T.sf[:], H[:, 0:1024])
+    g.vector.wait_ge(S.lx1, 16)
+    k_x1 = quant(T.qx[:, 256:512], T.sx[:, 256:512], T.xs[:, 1024:2048])
+    empty(H, 1024, 4, 4, c1)
+    own_first = members[a][0] < near[0]
+    po, pn = (1024, 1536) if own_first else (1536, 1024)
+    quant(T.qn[:], T.sn[:], H[:, pn:pn + 512])
+    k_h1 = quant(T.qb[:, bpair:bpair + 128], T.sb[:, bpair:bpair + 128], H[:, po:po + 512])
+    g.vector.wait_ge(S.lw2, 16)
+    k_w2 = quant(T.qw2[:], T.sw2[:], T.w2s[:])
+    g.vector.wait_ge(S.lw3, 16)
+    k_w3 = quant(T.qw3[:], T.sw3[:], T.w3s[:])
+    empty(G, 0, 0, 8, c2)
+    k_g0 = quant(T.qgf[:], T.sgf[:], G[:, 0:1024])
+    empty(G, 1024, 4, 12, c2)
+    k_g1 = quant(T.qa[:, apiece:apiece + 256], T.sa[:, apiece:apiece + 256], G[:, 1024:2048])
+
+    g.tensor.wait_ge(S.qv, k_a)
+    for i in range(4):
+        if i == 2:
+            g.tensor.wait_ge(S.qv, k_b)
+        g.tensor.matmul_mx(T.ps[:, 512 * i:512 * i + 256], T.qw1[:, 128 * i:128 * i + 128],
+                           T.sw1[:, 128 * i:128 * i + 128], T.qx[:, 0:256], T.sx[:, 0:256], True, True).then_inc(S.mm, 1)
+    g.tensor.wait_ge(S.qv, k_x1)
+    products(T.qw1, T.sw1, T.qx, T.sx, 256, 4)
+    g.tensor.wait_ge(S.qv, k_w2)
+    g.tensor.wait_ge(S.far1, 4 * 2 * (len(off) // 4))
+    products(T.qw2, T.sw2, T.qb, T.sb, bfar, 0)
+    n_near = 2 * 2 * (len(off) // 2) + 2 * (len(on) // 2)
+    g.tensor.wait_ge(S.near1, n_near)
+    products(T.qw2, T.sw2, T.qb, T.sb, bnear, 4)
+    g.tensor.wait_ge(S.qv, k_g0)
+    g.tensor.wait_ge(S.far2, 4 * 2 * (len(off) // 4))
+    for k in range(4):
+        if k == 2:
+            g.tensor.wait_ge(S.near2, n_near)
+            g.tensor.wait_ge(S.qv, k_g1)
+        c = (afar if k < 2 else anear) + 128 * (k % 2)
+        g.tensor.matmul_mx(T.ps[:, 512 * k:512 * k + 128], T.qw3[:], T.sw3[:], T.qa[:, c:c + 128], T.sa[:, c:c + 128],
+                           True, True).then_inc(S.mm, 1)
+
+    yfar, ynear = W * far[0], W * min(members[a][0], near[0])
+    ya, yn = W * members[a][0], W * near[0]
+    first, second = (ya, yn) if slot == 0 else (yn, ya)
+    for k, col in enumerate((yfar, yfar + 128, first, second)):
+        p = T.ps[:, 512 * k:512 * k + 128]
+        o = T.ys[:, col:col + 128]
+        if k % 2 == 0:
+            g.scalar.wait_ge(S.mm, 17 + k)
+            g.scalar.activation(o, p, ActivationFunctionType.Copy).then_inc(S.es, 1)
+            ns[0] += 1
+        else:
+            g.vector.wait_ge(S.mm, 17 + k)
+            g.vector.tensor_copy(o, p).then_inc(S.ev, 1)
+            nv[0] += 1
+            g.sync.wait_ge(S.es, ns[0])
+            g.sync.wait_ge(S.ev, nv[0])
+            q = yfar if k == 1 else ynear
+            g.sync.dma_start(T.y[:, q:q + 256], T.ys[:, q:q + 256]).then_inc(S.store, 16)
+    g.sync.wait_ge(S.store, 32)
+
+    B, A = ("qb", "sb"), ("qa", "sa")
+    g.wait_ge(S.qv, k_h0)
+    send([(d, share(off, i, 4), ("qf", "sf"), W * i, B, b_col(d, rank)) for i, d in enumerate(far)], S.far1)
+    g.wait_ge(S.qv, k_h1)
+    send([(d, share(off, i, 2), ("qn", "sn"), W * i, B, b_col(d, rank)) for i, d in enumerate(near)]
+         + [(partner, share(on, 0, 2), B, bpair + W * (1 - slot), B, b_col(partner, rank))], S.near1)
+    g.wait_ge(S.qv, k_g0)
+    send([(d, share(off, i, 4), ("qgf", "sgf"), W * i, A, a_col(d, rank)) for i, d in enumerate(far)], S.far2)
+    g.wait_ge(S.qv, k_g1)
+    p0, n0 = (apiece + 2 * W, apiece) if slot == 0 else (apiece + W, apiece + 2 * W)
+    send([(d, share(off, i, 2), A, n0 + W * i, A, a_col(d, rank)) for i, d in enumerate(near)]
+         + [(partner, share(on, 0, 2), A, p0, A, a_col(partner, rank))], S.near2)
+    g.wait_ge(S.sent, sent[0])

@@ -15,23 +15,22 @@ SCRATCH = {
     "qw1": ("sbuf", [128, 512], F8), "sw1": ("sbuf", [128, 512], "uint8"),
     "qw2": ("sbuf", [128, 512], F8), "sw2": ("sbuf", [128, 512], "uint8"),
     "qw3": ("sbuf", [128, 128], F8), "sw3": ("sbuf", [128, 128], "uint8"),
-    "qf": ("sbuf", [128, 256], F8), "sf": ("sbuf", [128, 256], "uint8"),
-    "qn": ("sbuf", [128, 128], F8), "sn": ("sbuf", [128, 128], "uint8"),
+    "qh": ("sbuf", [128, 384], F8), "sh": ("sbuf", [128, 384], "uint8"),
     "qb": ("sbuf", [128, 576], F8), "sb": ("sbuf", [128, 576], "uint8"),
-    "qgf": ("sbuf", [128, 256], F8), "sgf": ("sbuf", [128, 256], "uint8"),
+    "qg": ("sbuf", [128, 384], F8), "sg": ("sbuf", [128, 384], "uint8"),
     "qa": ("sbuf", [128, 704], F8), "sa": ("sbuf", [128, 704], "uint8"),
+    "qr1": ("sbuf", [128, 128], F8), "sr1": ("sbuf", [128, 128], "uint8"),
+    "qr2": ("sbuf", [128, 128], F8), "sr2": ("sbuf", [128, 128], "uint8"),
     "ps": ("psum", [128, 4096], "float32"),
 }
-SEMAPHORES = ["lx0", "lx1", "lw1a", "lw1b", "lw2", "lw3", "qv", "mm", "es", "ev", "sent",
-              "far1", "near1", "far2", "near2", "store"]
+SEMAPHORES = ["lxX", "lxN", "lxY", "lxO", "lw1a", "lw1b", "lw2", "lw3", "qv", "mm", "es", "ev", "sent", "store",
+              "rc1", "rs1", "rc2", "rs2", "X1", "N1", "Y1", "O1", "X2", "N2", "Y2"]
 
 
 def rank_program(g, core, T, topo):
-    rank = T.rank_of(core)
-    if rank is None:
-        return
     S = T.sem
     W = int(T.tables["CNT"][0][0])
+    P = 2 * W
     cores = T.cores
     chips = []
     for c in cores:
@@ -40,8 +39,8 @@ def rank_program(g, core, T, topo):
     members = [[r for r in range(len(cores)) if topo.chip(cores[r]) == ch] for ch in chips]
 
     def place(r):
-        a = chips.index(topo.chip(cores[r]))
-        return a, members[a].index(r)
+        i = chips.index(topo.chip(cores[r]))
+        return i, members[i].index(r)
 
     def far_of(r):
         base = 2 * (1 - place(r)[0] // 2)
@@ -50,8 +49,16 @@ def rank_program(g, core, T, topo):
     def near_of(r):
         return members[place(r)[0] ^ 1]
 
-    a, slot = place(rank)
-    far, near, partner = far_of(rank), near_of(rank), members[a][1 - slot]
+    def on_plane(r, yes):
+        mine = topo.chip(cores[r])
+        return [o for o in far_of(r) if topo.same_plane(mine, topo.chip(cores[o])) == yes]
+
+    def helper_of(r):
+        c0 = cores[r]
+        fit = [c for c in range(topo.CORES_PER_CHIP * topo.CHIPS)
+               if topo.chip(c) == topo.chip(c0) and topo.die(c) != topo.die(c0)
+               and all(topo.may_write(c, d) for d in cores)]
+        return fit[place(r)[1]]
 
     def b_col(r, o):
         s = place(r)[1]
@@ -69,15 +76,8 @@ def rank_program(g, core, T, topo):
             return (5 * W if s == 0 else 4 * W) + W * near_of(r).index(o)
         return 4 * W if s == 0 else 6 * W
 
-    bpair = 7 * W if slot == 0 else 0
-    bfar, bnear = (0, 4 * W) if slot == 0 else (5 * W, W)
-    apiece = 0 if slot == 0 else 7 * W
-    afar, anear = (7 * W, 3 * W) if slot == 0 else (0, 4 * W)
-
     def bits(m):
         return [1 << i for i in range(16) if m >> i & 1]
-    off = bits(topo.mask(core, cores[far[0]]))
-    on = [b for b in bits(topo.mask(core, cores[partner])) if b not in off]
 
     def share(engines, k, n):
         w = len(engines) // n
@@ -85,138 +85,182 @@ def rank_program(g, core, T, topo):
 
     sent = [0]
 
-    def send(moves, sem):
-        for part in (0, 1):
-            tr = []
-            for d, mask, src, sc, dst, dc in moves:
-                rid, pid, _ = topo.addr(cores[d])
-                s, t = T[src[part]][:, sc:sc + W], T[dst[part]][:, dc:dc + W]
-                if part == 0:
-                    s, t = s.bitcast(dt.uint8), t.bitcast(dt.uint8)
-                tr.append(RemoteDMATransfer(dst_ids=[DstId(rid=rid, pnc=pid)], dma_engine_mask=mask,
-                                            remote_sem=sem, src=s, dst=t))
-                sent[0] += len(bits(mask))
-            g.remote_dma_fused(tr, local_sem=S.sent)
+    def write(part, moves, sem):
+        tr = []
+        for d, mask, src, sc, dst, dc, n in moves:
+            rid, pid, _ = topo.addr(d)
+            s, t = T[src[part]][:, sc:sc + n], T[dst[part]][:, dc:dc + n]
+            if part == 0:
+                s, t = s.bitcast(dt.uint8), t.bitcast(dt.uint8)
+            tr.append(RemoteDMATransfer(dst_ids=[DstId(rid=rid, pnc=pid)], dma_engine_mask=mask, remote_sem=sem,
+                                        src=s, dst=t))
+            sent[0] += len(bits(mask))
+        g.remote_dma_fused(tr, local_sem=S.sent)
 
-    fx = 4 * W * far[0]
-    nx = 4 * W * min(members[a][0], near[0])
-    g.sync.dma_start(T.xs[:, 0:1024], T.x[:, fx:fx + 1024]).then_inc(S.lx0, 16)
+    QH, QG, B, A, R1, R2 = ("qh", "sh"), ("qg", "sg"), ("qb", "sb"), ("qa", "sa"), ("qr1", "sr1"), ("qr2", "sr2")
+    rank = T.rank_of(core)
+    if rank is None:
+        for r in range(len(cores)):
+            if helper_of(r) == core:
+                to_x, to_n = on_plane(r, False), near_of(r)
+                out = bits(topo.mask(core, cores[to_x[0]]))
+                for sems, dests, buf, dst, col, sem in ((("rc1", "rs1"), to_x, R1, B, b_col, S.X1),
+                                                        (("rc2", "rs2"), to_n, R2, A, a_col, S.N2)):
+                    for part in (0, 1):
+                        g.wait_ge(S[sems[part]], 4)
+                        write(part, [(cores[d], share(out, i, 2), buf, W * i, dst, col(d, r), W)
+                                     for i, d in enumerate(dests)], sem)
+                g.wait_ge(S.sent, sent[0])
+        return
+
+    a, slot = place(rank)
+    near, partner, helper = near_of(rank), members[a][1 - slot], helper_of(rank)
+    to_x, to_y = on_plane(rank, False), on_plane(rank, True)
+    off = bits(topo.mask(core, cores[to_x[0]]))
+    on = [b for b in bits(topo.mask(core, helper)) if b not in off]
+    bpair, bown = (7 * W, 6 * W) if slot == 0 else (0, W)
+    apair, aown = (2 * W, 3 * W) if slot == 0 else (7 * W, 6 * W)
+
+    xcol = {"X": W * to_x[0], "N": W * near[0], "Y": W * to_y[0], "O": W * members[a][0]}
+    order1, order2 = ("X", "N", "Y", "O"), ("N", "Y", "X", "O")
+    E = 4 * P
+
+    def load_x(q, p):
+        i = E * order1.index(p)
+        q.dma_start(T.xs[:, i:i + E], T.x[:, 4 * xcol[p]:4 * xcol[p] + E]).then_inc(S["lx" + p], 16)
+
+    load_x(g.sync, "X")
     g.scalar.dma_start(T.w1s[:, 0:1024], T.w1[:, 0:1024]).then_inc(S.lw1a, 16)
     g.sync.dma_start(T.w1s[:, 1024:2048], T.w1[:, 1024:2048]).then_inc(S.lw1b, 16)
-    g.scalar.dma_start(T.xs[:, 1024:2048], T.x[:, nx:nx + 1024]).then_inc(S.lx1, 16)
+    load_x(g.scalar, "N")
+    load_x(g.sync, "Y")
+    load_x(g.scalar, "O")
     g.sync.dma_start(T.w2s[:], T.w2[:]).then_inc(S.lw2, 16)
     g.scalar.dma_start(T.w3s[:], T.w3[:]).then_inc(S.lw3, 16)
 
-    nq, nm, ns, nv = [0], [0], [0], [0]
+    nq, ns, nv = [0], [0], [0]
 
     def quant(codes, scales, src):
         g.vector.quantize_mx(codes, scales, src).then_inc(S.qv, 1)
         nq[0] += 1
         return nq[0]
 
-    def products(w, sw, x, sx, c, bank):
-        for i in range(4):
-            p = 512 * (bank + i)
-            g.tensor.matmul_mx(T.ps[:, p:p + 256], w[:, 128 * i:128 * i + 128], sw[:, 128 * i:128 * i + 128],
-                               x[:, c:c + 256], sx[:, c:c + 256], True, True).then_inc(S.mm, 1)
+    def quant_x(p):
+        i = order1.index(p)
+        g.vector.wait_ge(S["lx" + p], 16)
+        return quant(T.qx[:, P * i:P * i + P], T.sx[:, P * i:P * i + P], T.xs[:, E * i:E * i + E])
 
-    def empty(t, lo, bank, m0, c):
-        for i in (0, 2):
+    def products(w, sw, x, sx, c, bank, which=(0, 1, 2, 3)):
+        for i in which:
             p = 512 * (bank + i)
-            g.scalar.wait_ge(S.mm, m0 + i + 1)
-            g.scalar.activation(t[:, lo + i:lo + 1024:4], T.ps[:, p:p + 256], ActivationFunctionType.Relu,
-                                scale=c).then_inc(S.es, 1)
-            ns[0] += 1
-        for i in (1, 3):
-            p = 512 * (bank + i)
-            g.vector.wait_ge(S.mm, m0 + i + 1)
-            g.vector.tensor_scalar(t[:, lo + i:lo + 1024:4], T.ps[:, p:p + 256], 0.0, c, AluOpType.max,
-                                   AluOpType.mult).then_inc(S.ev, 1)
-            nv[0] += 1
+            g.tensor.matmul_mx(T.ps[:, p:p + P], w[:, 128 * i:128 * i + 128], sw[:, 128 * i:128 * i + 128],
+                               x[:, c:c + P], sx[:, c:c + P], True, True).then_inc(S.mm, 1)
+
+    def empty(t, k, bank, m0, c, by_scalar):
+        for i in range(4):
+            p, w = 512 * (bank + i), slice(E * k + i, E * k + E, 4)
+            if i in by_scalar:
+                g.scalar.wait_ge(S.mm, m0 + i + 1)
+                g.scalar.activation(t[:, w], T.ps[:, p:p + P], ActivationFunctionType.Relu, scale=c).then_inc(S.es, 1)
+                ns[0] += 1
+            else:
+                g.vector.wait_ge(S.mm, m0 + i + 1)
+                g.vector.tensor_scalar(t[:, w], T.ps[:, p:p + P], 0.0, c, AluOpType.max, AluOpType.mult).then_inc(S.ev, 1)
+                nv[0] += 1
         g.vector.wait_ge(S.es, ns[0])
         g.vector.wait_ge(S.ev, nv[0])
 
     c1, c2 = float(np.float32(0.043)), float(np.float32(0.047))
-    H, G = T.h, T.gt
 
-    g.vector.wait_ge(S.lx0, 16)
-    quant(T.qx[:, 0:256], T.sx[:, 0:256], T.xs[:, 0:1024])
+    kx, kh, kg = {}, {}, {}
+    kx["X"] = quant_x("X")
     g.vector.wait_ge(S.lw1a, 16)
     k_a = quant(T.qw1[:, 0:256], T.sw1[:, 0:256], T.w1s[:, 0:1024])
     g.vector.wait_ge(S.lw1b, 16)
     k_b = quant(T.qw1[:, 256:512], T.sw1[:, 256:512], T.w1s[:, 1024:2048])
-    empty(H, 0, 0, 0, c1)
-    k_h0 = quant(T.qf[:], T.sf[:], H[:, 0:1024])
-    g.vector.wait_ge(S.lx1, 16)
-    k_x1 = quant(T.qx[:, 256:512], T.sx[:, 256:512], T.xs[:, 1024:2048])
-    empty(H, 1024, 4, 4, c1)
-    own_first = members[a][0] < near[0]
-    po, pn = (1024, 1536) if own_first else (1536, 1024)
-    quant(T.qn[:], T.sn[:], H[:, pn:pn + 512])
-    k_h1 = quant(T.qb[:, bpair:bpair + 128], T.sb[:, bpair:bpair + 128], H[:, po:po + 512])
+    for k, p in enumerate(order1):
+        if k < 3:
+            kx[order1[k + 1]] = quant_x(order1[k + 1])
+        empty(T.h, k, 4 * (k % 2), 4 * k, c1, (0, 1, 3))
+        q, s, c = (T.qb, T.sb, bpair) if p == "O" else (T.qh, T.sh, P * k)
+        kh[p] = quant(q[:, c:c + P], s[:, c:c + P], T.h[:, E * k:E * k + E])
     g.vector.wait_ge(S.lw2, 16)
     k_w2 = quant(T.qw2[:], T.sw2[:], T.w2s[:])
     g.vector.wait_ge(S.lw3, 16)
-    k_w3 = quant(T.qw3[:], T.sw3[:], T.w3s[:])
-    empty(G, 0, 0, 8, c2)
-    k_g0 = quant(T.qgf[:], T.sgf[:], G[:, 0:1024])
-    empty(G, 1024, 4, 12, c2)
-    k_g1 = quant(T.qa[:, apiece:apiece + 256], T.sa[:, apiece:apiece + 256], G[:, 1024:2048])
+    quant(T.qw3[:], T.sw3[:], T.w3s[:])
+    for k, p in enumerate(order2):
+        empty(T.gt, k, 4 * (k % 2), 16 + 4 * k, c2, (0, 2))
+        q, s, c = (T.qa, T.sa, apair) if p == "O" else (T.qg, T.sg, P * k)
+        kg[p] = quant(q[:, c:c + P], s[:, c:c + P], T.gt[:, E * k:E * k + E])
 
-    g.tensor.wait_ge(S.qv, k_a)
-    for i in range(4):
-        if i == 2:
+    n_off, n_on = 2 * len(off), 8
+    for k, p in enumerate(order1):
+        if k == 0:
+            g.tensor.wait_ge(S.qv, k_a)
+            products(T.qw1, T.sw1, T.qx, T.sx, 0, 0, (0, 1))
             g.tensor.wait_ge(S.qv, k_b)
-        g.tensor.matmul_mx(T.ps[:, 512 * i:512 * i + 256], T.qw1[:, 128 * i:128 * i + 128],
-                           T.sw1[:, 128 * i:128 * i + 128], T.qx[:, 0:256], T.sx[:, 0:256], True, True).then_inc(S.mm, 1)
-    g.tensor.wait_ge(S.qv, k_x1)
-    products(T.qw1, T.sw1, T.qx, T.sx, 256, 4)
-    g.tensor.wait_ge(S.qv, k_w2)
-    g.tensor.wait_ge(S.far1, 4 * 2 * (len(off) // 4))
-    products(T.qw2, T.sw2, T.qb, T.sb, bfar, 0)
-    n_near = 2 * 2 * (len(off) // 2) + 2 * (len(on) // 2)
-    g.tensor.wait_ge(S.near1, n_near)
-    products(T.qw2, T.sw2, T.qb, T.sb, bnear, 4)
-    g.tensor.wait_ge(S.qv, k_g0)
-    g.tensor.wait_ge(S.far2, 4 * 2 * (len(off) // 4))
-    for k in range(4):
-        if k == 2:
-            g.tensor.wait_ge(S.near2, n_near)
-            g.tensor.wait_ge(S.qv, k_g1)
-        c = (afar if k < 2 else anear) + 128 * (k % 2)
-        g.tensor.matmul_mx(T.ps[:, 512 * k:512 * k + 128], T.qw3[:], T.sw3[:], T.qa[:, c:c + 128], T.sa[:, c:c + 128],
+            products(T.qw1, T.sw1, T.qx, T.sx, 0, 0, (2, 3))
+        else:
+            g.tensor.wait_ge(S.qv, max(kx[p], kh[order1[k - 2]] if k > 1 else 0))
+            products(T.qw1, T.sw1, T.qx, T.sx, P * k, 4 * (k % 2))
+    bcol = {"X": b_col(rank, to_x[0]), "N": b_col(rank, near[0]), "Y": b_col(rank, to_y[0]), "O": bown}
+    for k, p in enumerate(order2):
+        g.tensor.wait_ge(S.qv, kg[order2[k - 2]] if k > 1 else k_w2)
+        g.tensor.wait_ge(S[p + "1"], n_on if p == "O" else n_off)
+        products(T.qw2, T.sw2, T.qb, T.sb, bcol[p], 4 * (k % 2))
+    g.tensor.wait_ge(S.qv, kg["X"])
+    acol = {"X": a_col(rank, to_x[0]), "N": a_col(rank, near[0]), "Y": a_col(rank, to_y[0]), "O": aown}
+    for k, p in enumerate(("Y", "N", "O", "X")):
+        if p == "N":
+            g.tensor.wait_ge(S.N2, n_off + n_on)
+            g.tensor.wait_ge(S.qv, kg["O"])
+        elif p != "O":
+            g.tensor.wait_ge(S[p + "2"], n_off)
+        b, o = T.ps[:, 512 * k:512 * k + P], T.ys[:, xcol[p]:xcol[p] + P]
+        g.tensor.matmul_mx(b, T.qw3[:], T.sw3[:], T.qa[:, acol[p]:acol[p] + P], T.sa[:, acol[p]:acol[p] + P],
                            True, True).then_inc(S.mm, 1)
-
-    yfar, ynear = W * far[0], W * min(members[a][0], near[0])
-    ya, yn = W * members[a][0], W * near[0]
-    first, second = (ya, yn) if slot == 0 else (yn, ya)
-    for k, col in enumerate((yfar, yfar + 128, first, second)):
-        p = T.ps[:, 512 * k:512 * k + 128]
-        o = T.ys[:, col:col + 128]
         if k % 2 == 0:
-            g.scalar.wait_ge(S.mm, 17 + k)
-            g.scalar.activation(o, p, ActivationFunctionType.Copy).then_inc(S.es, 1)
+            g.scalar.wait_ge(S.mm, 33 + k)
+            g.scalar.activation(o, b, ActivationFunctionType.Copy).then_inc(S.es, 1)
             ns[0] += 1
         else:
-            g.vector.wait_ge(S.mm, 17 + k)
-            g.vector.tensor_copy(o, p).then_inc(S.ev, 1)
+            g.vector.wait_ge(S.mm, 33 + k)
+            g.vector.tensor_copy(o, b).then_inc(S.ev, 1)
             nv[0] += 1
+        if k >= 2:
             g.sync.wait_ge(S.es, ns[0])
             g.sync.wait_ge(S.ev, nv[0])
-            q = yfar if k == 1 else ynear
-            g.sync.dma_start(T.y[:, q:q + 256], T.ys[:, q:q + 256]).then_inc(S.store, 16)
+            c = min(xcol["N"], xcol["O"]) if k == 2 else min(xcol["X"], xcol["Y"])
+            g.sync.dma_start(T.y[:, c:c + 2 * P], T.ys[:, c:c + 2 * P]).then_inc(S.store, 16)
     g.sync.wait_ge(S.store, 32)
 
-    B, A = ("qb", "sb"), ("qa", "sa")
-    g.wait_ge(S.qv, k_h0)
-    send([(d, share(off, i, 4), ("qf", "sf"), W * i, B, b_col(d, rank)) for i, d in enumerate(far)], S.far1)
-    g.wait_ge(S.qv, k_h1)
-    send([(d, share(off, i, 2), ("qn", "sn"), W * i, B, b_col(d, rank)) for i, d in enumerate(near)]
-         + [(partner, share(on, 0, 2), B, bpair + W * (1 - slot), B, b_col(partner, rank))], S.near1)
-    g.wait_ge(S.qv, k_g0)
-    send([(d, share(off, i, 4), ("qgf", "sgf"), W * i, A, a_col(d, rank)) for i, d in enumerate(far)], S.far2)
-    g.wait_ge(S.qv, k_g1)
-    p0, n0 = (apiece + 2 * W, apiece) if slot == 0 else (apiece + W, apiece + 2 * W)
-    send([(d, share(off, i, 2), A, n0 + W * i, A, a_col(d, rank)) for i, d in enumerate(near)]
-         + [(partner, share(on, 0, 2), A, p0, A, a_col(partner, rank))], S.near2)
+    def relay(src, k, buf, sems):
+        for part in (0, 1):
+            write(part, [(helper, share(on, 0, 2), src, P * k, buf, 0, P)], S[sems[part]])
+
+    def direct(dests, src, k, dst, col, sem):
+        for part in (0, 1):
+            write(part, [(cores[d], share(off, i, 2), src, P * k + W * i, dst, col(d, rank), W)
+                         for i, d in enumerate(dests)], sem)
+
+    def to_partner(buf, c, col, sem):
+        for part in (0, 1):
+            write(part, [(cores[partner], share(on, 0, 2), buf, c, buf, col(partner, rank), W)], sem)
+
+    g.wait_ge(S.qv, kh["X"])
+    relay(QH, 0, R1, ("rc1", "rs1"))
+    g.wait_ge(S.qv, kh["N"])
+    direct(near, QH, 1, B, b_col, S.N1)
+    g.wait_ge(S.qv, kh["Y"])
+    direct(to_y, QH, 2, B, b_col, S.Y1)
+    g.wait_ge(S.qv, kh["O"])
+    to_partner(B, bpair + W * (1 - slot), b_col, S.O1)
+    g.wait_ge(S.qv, kg["N"])
+    relay(QG, 0, R2, ("rc2", "rs2"))
+    g.wait_ge(S.qv, kg["Y"])
+    direct(to_y, QG, 1, A, a_col, S.Y2)
+    g.wait_ge(S.qv, kg["X"])
+    direct(to_x, QG, 2, A, a_col, S.X2)
+    g.wait_ge(S.qv, kg["O"])
+    to_partner(A, apair + W * slot, a_col, S.N2)
     g.wait_ge(S.sent, sent[0])

import numpy as np
from concourse.bass import DstId, RemoteDMATransfer
from concourse.mybir import dt, AluOpType, ActivationFunctionType

F8 = "float8_e4m3fn_x4"
SCRATCH = {
    "xs": ("sbuf", [128, 2048], "bfloat16"),
    "w1s": ("sbuf", [128, 2048], "bfloat16"),
    "w2s": ("sbuf", [128, 2048], "bfloat16"),
    "w3s": ("sbuf", [128, 512], "bfloat16"),
    "h": ("sbuf", [128, 2048], "bfloat16"),
    "gt": ("sbuf", [128, 2048], "bfloat16"),
    "ys": ("sbuf", [128, 512], "float32"),
    "qx": ("sbuf", [128, 512], F8), "sx": ("sbuf", [128, 512], "uint8"),
    "qw1": ("sbuf", [128, 512], F8), "sw1": ("sbuf", [128, 512], "uint8"),
    "qw2": ("sbuf", [128, 512], F8), "sw2": ("sbuf", [128, 512], "uint8"),
    "qw3": ("sbuf", [128, 128], F8), "sw3": ("sbuf", [128, 128], "uint8"),
    "qh": ("sbuf", [128, 384], F8), "sh": ("sbuf", [128, 384], "uint8"),
    "qb": ("sbuf", [128, 576], F8), "sb": ("sbuf", [128, 576], "uint8"),
    "qg": ("sbuf", [128, 384], F8), "sg": ("sbuf", [128, 384], "uint8"),
    "qa": ("sbuf", [128, 704], F8), "sa": ("sbuf", [128, 704], "uint8"),
    "qr1": ("sbuf", [128, 128], F8), "sr1": ("sbuf", [128, 128], "uint8"),
    "qr2": ("sbuf", [128, 128], F8), "sr2": ("sbuf", [128, 128], "uint8"),
    "ps": ("psum", [128, 4096], "float32"),
}
SEMAPHORES = ["lxX", "lxN", "lxY", "lxO", "lw1a", "lw1b", "lw2", "lw3", "qv", "mm", "es", "ev", "sent", "store",
              "rc1", "rs1", "rc2", "rs2", "X1", "N1", "Y1", "O1", "X2", "N2", "Y2"]


def rank_program(g, core, T, topo):
    S = T.sem
    W = int(T.tables["CNT"][0][0])
    P = 2 * W
    cores = T.cores
    chips = []
    for c in cores:
        if topo.chip(c) not in chips:
            chips.append(topo.chip(c))
    members = [[r for r in range(len(cores)) if topo.chip(cores[r]) == ch] for ch in chips]

    def place(r):
        i = chips.index(topo.chip(cores[r]))
        return i, members[i].index(r)

    def far_of(r):
        base = 2 * (1 - place(r)[0] // 2)
        return members[base] + members[base + 1]

    def near_of(r):
        return members[place(r)[0] ^ 1]

    def on_plane(r, yes):
        mine = topo.chip(cores[r])
        return [o for o in far_of(r) if topo.same_plane(mine, topo.chip(cores[o])) == yes]

    def helper_of(r):
        c0 = cores[r]
        fit = [c for c in range(topo.CORES_PER_CHIP * topo.CHIPS)
               if topo.chip(c) == topo.chip(c0) and topo.die(c) != topo.die(c0)
               and all(topo.may_write(c, d) for d in cores)]
        return fit[place(r)[1]]

    def b_col(r, o):
        s = place(r)[1]
        if o in far_of(r):
            return (0 if s == 0 else 5 * W) + W * far_of(r).index(o)
        if o in near_of(r):
            return (4 * W if s == 0 else 3 * W) + W * near_of(r).index(o)
        return 6 * W if s == 0 else 2 * W

    def a_col(r, o):
        s = place(r)[1]
        if o in far_of(r):
            return (7 * W if s == 0 else 0) + W * far_of(r).index(o)
        if o in near_of(r):
            return (5 * W if s == 0 else 4 * W) + W * near_of(r).index(o)
        return 4 * W if s == 0 else 6 * W

    def bits(m):
        return [1 << i for i in range(16) if m >> i & 1]

    def share(engines, k, n):
        w = len(engines) // n
        return sum(engines[k * w:k * w + w])

    sent = [0]

    def write(part, moves, sem):
        tr = []
        for d, mask, src, sc, dst, dc, n in moves:
            rid, pid, _ = topo.addr(d)
            s, t = T[src[part]][:, sc:sc + n], T[dst[part]][:, dc:dc + n]
            if part == 0:
                s, t = s.bitcast(dt.uint8), t.bitcast(dt.uint8)
            tr.append(RemoteDMATransfer(dst_ids=[DstId(rid=rid, pnc=pid)], dma_engine_mask=mask, remote_sem=sem,
                                        src=s, dst=t))
            sent[0] += len(bits(mask))
        g.remote_dma_fused(tr, local_sem=S.sent)

    QH, QG, B, A, R1, R2 = ("qh", "sh"), ("qg", "sg"), ("qb", "sb"), ("qa", "sa"), ("qr1", "sr1"), ("qr2", "sr2")
    rank = T.rank_of(core)
    if rank is None:
        for r in range(len(cores)):
            if helper_of(r) == core:
                to_x, to_n = on_plane(r, False), near_of(r)
                out = bits(topo.mask(core, cores[to_x[0]]))
                for sems, dests, buf, dst, col, sem in ((("rc1", "rs1"), to_x, R1, B, b_col, S.X1),
                                                        (("rc2", "rs2"), to_n, R2, A, a_col, S.N2)):
                    for part in (0, 1):
                        g.wait_ge(S[sems[part]], 4)
                        write(part, [(cores[d], share(out, i, 2), buf, W * i, dst, col(d, r), W)
                                     for i, d in enumerate(dests)], sem)
                g.wait_ge(S.sent, sent[0])
        return

    a, slot = place(rank)
    near, partner, helper = near_of(rank), members[a][1 - slot], helper_of(rank)
    to_x, to_y = on_plane(rank, False), on_plane(rank, True)
    off = bits(topo.mask(core, cores[to_x[0]]))
    on = [b for b in bits(topo.mask(core, helper)) if b not in off]
    bpair, bown = (7 * W, 6 * W) if slot == 0 else (0, W)
    apair, aown = (2 * W, 3 * W) if slot == 0 else (7 * W, 6 * W)

    xcol = {"X": W * to_x[0], "N": W * near[0], "Y": W * to_y[0], "O": W * members[a][0]}
    order1, order2 = ("X", "N", "Y", "O"), ("N", "Y", "X", "O")
    E = 4 * P

    def load_x(q, p):
        i = E * order1.index(p)
        q.dma_start(T.xs[:, i:i + E], T.x[:, 4 * xcol[p]:4 * xcol[p] + E]).then_inc(S["lx" + p], 16)

    load_x(g.sync, "X")
    g.scalar.dma_start(T.w1s[:, 0:1024], T.w1[:, 0:1024]).then_inc(S.lw1a, 16)
    g.sync.dma_start(T.w1s[:, 1024:2048], T.w1[:, 1024:2048]).then_inc(S.lw1b, 16)
    load_x(g.scalar, "N")
    load_x(g.sync, "Y")
    load_x(g.scalar, "O")
    g.sync.dma_start(T.w2s[:], T.w2[:]).then_inc(S.lw2, 16)
    g.scalar.dma_start(T.w3s[:], T.w3[:]).then_inc(S.lw3, 16)

    nq, ns, nv = [0], [0], [0]

    def quant(codes, scales, src):
        g.vector.quantize_mx(codes, scales, src).then_inc(S.qv, 1)
        nq[0] += 1
        return nq[0]

    def quant_x(p):
        i = order1.index(p)
        g.vector.wait_ge(S["lx" + p], 16)
        return quant(T.qx[:, P * i:P * i + P], T.sx[:, P * i:P * i + P], T.xs[:, E * i:E * i + E])

    def products(w, sw, x, sx, c, bank, which=(0, 1, 2, 3)):
        for i in which:
            p = 512 * (bank + i)
            g.tensor.matmul_mx(T.ps[:, p:p + P], w[:, 128 * i:128 * i + 128], sw[:, 128 * i:128 * i + 128],
                               x[:, c:c + P], sx[:, c:c + P], True, True).then_inc(S.mm, 1)

    def empty(t, k, bank, m0, c, by_scalar):
        for i in range(4):
            p, w = 512 * (bank + i), slice(E * k + i, E * k + E, 4)
            if i in by_scalar:
                g.scalar.wait_ge(S.mm, m0 + i + 1)
                g.scalar.activation(t[:, w], T.ps[:, p:p + P], ActivationFunctionType.Relu, scale=c).then_inc(S.es, 1)
                ns[0] += 1
            else:
                g.vector.wait_ge(S.mm, m0 + i + 1)
                g.vector.tensor_scalar(t[:, w], T.ps[:, p:p + P], 0.0, c, AluOpType.max, AluOpType.mult).then_inc(S.ev, 1)
                nv[0] += 1
        g.vector.wait_ge(S.es, ns[0])
        g.vector.wait_ge(S.ev, nv[0])

    c1, c2 = float(np.float32(0.043)), float(np.float32(0.047))

    kx, kh, kg = {}, {}, {}
    kx["X"] = quant_x("X")
    g.vector.wait_ge(S.lw1a, 16)
    k_a = quant(T.qw1[:, 0:256], T.sw1[:, 0:256], T.w1s[:, 0:1024])
    g.vector.wait_ge(S.lw1b, 16)
    k_b = quant(T.qw1[:, 256:512], T.sw1[:, 256:512], T.w1s[:, 1024:2048])
    for k, p in enumerate(order1):
        if k < 3:
            kx[order1[k + 1]] = quant_x(order1[k + 1])
        empty(T.h, k, 4 * (k % 2), 4 * k, c1, (0, 1, 3))
        q, s, c = (T.qb, T.sb, bpair) if p == "O" else (T.qh, T.sh, P * k)
        kh[p] = quant(q[:, c:c + P], s[:, c:c + P], T.h[:, E * k:E * k + E])
    g.vector.wait_ge(S.lw2, 16)
    k_w2 = quant(T.qw2[:], T.sw2[:], T.w2s[:])
    g.vector.wait_ge(S.lw3, 16)
    quant(T.qw3[:], T.sw3[:], T.w3s[:])
    for k, p in enumerate(order2):
        empty(T.gt, k, 4 * (k % 2), 16 + 4 * k, c2, (0, 2))
        q, s, c = (T.qa, T.sa, apair) if p == "O" else (T.qg, T.sg, P * k)
        kg[p] = quant(q[:, c:c + P], s[:, c:c + P], T.gt[:, E * k:E * k + E])

    n_off, n_on = 2 * len(off), 8
    for k, p in enumerate(order1):
        if k == 0:
            g.tensor.wait_ge(S.qv, k_a)
            products(T.qw1, T.sw1, T.qx, T.sx, 0, 0, (0, 1))
            g.tensor.wait_ge(S.qv, k_b)
            products(T.qw1, T.sw1, T.qx, T.sx, 0, 0, (2, 3))
        else:
            g.tensor.wait_ge(S.qv, max(kx[p], kh[order1[k - 2]] if k > 1 else 0))
            products(T.qw1, T.sw1, T.qx, T.sx, P * k, 4 * (k % 2))
    bcol = {"X": b_col(rank, to_x[0]), "N": b_col(rank, near[0]), "Y": b_col(rank, to_y[0]), "O": bown}
    for k, p in enumerate(order2):
        g.tensor.wait_ge(S.qv, kg[order2[k - 2]] if k > 1 else k_w2)
        g.tensor.wait_ge(S[p + "1"], n_on if p == "O" else n_off)
        products(T.qw2, T.sw2, T.qb, T.sb, bcol[p], 4 * (k % 2))
    g.tensor.wait_ge(S.qv, kg["X"])
    acol = {"X": a_col(rank, to_x[0]), "N": a_col(rank, near[0]), "Y": a_col(rank, to_y[0]), "O": aown}
    for k, p in enumerate(("Y", "N", "O", "X")):
        if p == "N":
            g.tensor.wait_ge(S.N2, n_off + n_on)
            g.tensor.wait_ge(S.qv, kg["O"])
        elif p != "O":
            g.tensor.wait_ge(S[p + "2"], n_off)
        b, o = T.ps[:, 512 * k:512 * k + P], T.ys[:, xcol[p]:xcol[p] + P]
        g.tensor.matmul_mx(b, T.qw3[:], T.sw3[:], T.qa[:, acol[p]:acol[p] + P], T.sa[:, acol[p]:acol[p] + P],
                           True, True).then_inc(S.mm, 1)
        if k % 2 == 0:
            g.scalar.wait_ge(S.mm, 33 + k)
            g.scalar.activation(o, b, ActivationFunctionType.Copy).then_inc(S.es, 1)
            ns[0] += 1
        else:
            g.vector.wait_ge(S.mm, 33 + k)
            g.vector.tensor_copy(o, b).then_inc(S.ev, 1)
            nv[0] += 1
        if k >= 2:
            g.sync.wait_ge(S.es, ns[0])
            g.sync.wait_ge(S.ev, nv[0])
            c = min(xcol["N"], xcol["O"]) if k == 2 else min(xcol["X"], xcol["Y"])
            g.sync.dma_start(T.y[:, c:c + 2 * P], T.ys[:, c:c + 2 * P]).then_inc(S.store, 16)
    g.sync.wait_ge(S.store, 32)

    def relay(src, k, buf, sems):
        for part in (0, 1):
            write(part, [(helper, share(on, 0, 2), src, P * k, buf, 0, P)], S[sems[part]])

    def direct(dests, src, k, dst, col, sem):
        for part in (0, 1):
            write(part, [(cores[d], share(off, i, 2), src, P * k + W * i, dst, col(d, rank), W)
                         for i, d in enumerate(dests)], sem)

    def to_partner(buf, c, col, sem):
        for part in (0, 1):
            write(part, [(cores[partner], share(on, 0, 2), buf, c, buf, col(partner, rank), W)], sem)

    g.wait_ge(S.qv, kh["X"])
    relay(QH, 0, R1, ("rc1", "rs1"))
    g.wait_ge(S.qv, kh["N"])
    direct(near, QH, 1, B, b_col, S.N1)
    g.wait_ge(S.qv, kh["Y"])
    direct(to_y, QH, 2, B, b_col, S.Y1)
    g.wait_ge(S.qv, kh["O"])
    to_partner(B, bpair + W * (1 - slot), b_col, S.O1)
    g.wait_ge(S.qv, kg["N"])
    relay(QG, 0, R2, ("rc2", "rs2"))
    g.wait_ge(S.qv, kg["Y"])
    direct(to_y, QG, 1, A, a_col, S.Y2)
    g.wait_ge(S.qv, kg["X"])
    direct(to_x, QG, 2, A, a_col, S.X2)
    g.wait_ge(S.qv, kg["O"])
    to_partner(A, apair + W * slot, a_col, S.N2)
    g.wait_ge(S.sent, sent[0])
